import numpy as np, ml_dtypes
CORES = [3,11,19,27,35,43,51,59]
N = 8
import mx_ref
BF = ml_dtypes.bfloat16
def gentries(a):
    return np.ascontiguousarray(a.reshape(8, 16, -1).transpose(0, 2, 1)).reshape(8, -1)
def gtable(e):
    e = np.asarray(e); return np.ascontiguousarray(e.reshape(8, -1, 16).transpose(0, 2, 1)).reshape(128, -1).astype(np.int32)
def gcols(t, e):
    v = np.concatenate([t.reshape(8, 16, -1, 4), np.zeros((8, 16, 1, 4), BF)], axis=2)
    return np.ascontiguousarray(np.stack([v[g][:, e[g]] for g in range(8)])).reshape(128, -1)
def tile(rs):
    return np.stack(rs, axis=2).reshape(128, -1).astype(BF)
def pick(q, e):
    c = np.concatenate([q[0].reshape(128, -1, 4), np.zeros((128, 1, 4), np.uint8)], axis=1); s = np.concatenate([q[1], np.ones((16, 1), np.uint8)], axis=1)
    return (np.ascontiguousarray(c[:, e].reshape(128, -1)), np.ascontiguousarray(s[:, e]))
def join(*qs):
    return (np.concatenate([q[0] for q in qs], axis=1), np.concatenate([q[1] for q in qs], axis=1))
def put(q, e, v):
    c, s = q[0].reshape(128, -1, 4).copy(), q[1].copy(); c[:, e] = v[0].reshape(128, -1, 4); s[:, e] = v[1]
    return (c.reshape(128, -1), s)
def pk(c, s):
    return (np.ascontiguousarray(c), mx_ref.live(s))
def emit(q):
    return q[0], q[1]
def packed(v, rng):
    q = [mx_ref.quantize(np.ascontiguousarray(v[r])) for r in range(N)]
    return np.stack([a for a, b in q]), np.stack([mx_ref.plane(b, rng) for a, b in q])
def values_of_codes():
    e, c = np.zeros((128, 128, 4), np.float32), np.zeros((128, 2, 4), np.uint8)
    e[np.arange(128), np.arange(128), 0] = 1
    c[:127, :, 0] = np.arange(256).reshape(2, 128).T[:127]
    return mx_ref.matmul(mx_ref.quantize(e.reshape(128, 512).astype(BF)), (c.reshape(128, 8), np.full((16, 2), 127, np.uint8))).T.reshape(-1).astype(np.float64)
CODE_VALUE, SCALE_VALUE = values_of_codes(), 2.0 ** (np.arange(256) - 127.0)
def decode(q):
    return (CODE_VALUE[q[0]].reshape(16, 8, -1, 4) * SCALE_VALUE[q[1]][:, None, :, None] + 0.0).reshape(128, -1).astype(np.float32)
def f(rng, *shape):
    return mx_ref.flush((rng.standard_normal(shape, dtype=np.float32) * np.exp2(rng.integers(-2, 3, shape[:-1] + (1,)))).astype(BF))
def wide(rng, *shape, cols=0):
    v = rng.standard_normal(shape, dtype=np.float32) * np.exp2(rng.integers(-12, 13, shape)).astype(np.float32)
    if cols: v *= np.repeat(np.exp2(rng.integers(-cols, cols + 1, shape[:-2] + (1, shape[-1] // 4))) * (rng.random(shape[:-2] + (1, shape[-1] // 4)) > 0.0625), 4, axis=-1).astype(np.float32)
    return mx_ref.flush(v.astype(BF))
C, T, R = 384, 192, 3
STEP = [1, 2, 4]
def big(v):
    v = v.astype(np.float32)
    v[np.abs(v) < np.float32(2.0 ** -16)] = 0
    return v.astype(BF)
def numbers_of(rng):
    return {"x": big(f(rng, N, 128, 4 * C)), "bm": big(f(rng, N, 128, 4 * C)), "u": np.array(f(rng, N, 128, 512)), "v": np.array(f(rng, N, 128, 512))}
def stored(a):
    return {"co": np.stack([gtable(e) for e in a]), "cn": np.stack([gtable(np.concatenate([a[(r + s) % N][:, :T] for s in STEP], axis=1)) for r in range(N)])}
def anywhere(rng):
    return rng.integers(0, C, (N, 8, C))
def weights(rng, w):
    c, p = packed(w, rng)
    return {"wc": c, "ws": p}
def straight(rng, size):
    w = np.zeros((N, 128, 4, 128, 4), np.float32)
    i = np.arange(128)
    for k in range(4): w[:, i, k, i, k] = np.tile(size, 8)
    return weights(rng, w.reshape(N, 128, 2048).astype(BF))
def signs(rng):
    return np.stack([rng.permutation(8) % 2 * 2.0 - 1.0 for r in range(N)])
def setup_inputs(rng):
    return {**numbers_of(rng), **stored(anywhere(rng)), **weights(rng, f(rng, N, 128, 2048))}
def setup_inputs_ties(rng):
    d = numbers_of(rng)
    e = rng.permutation(N)
    x = d["x"].reshape(N, 8, 16, C, 4)
    bm = d["bm"].reshape(N, 8, 16, C, 4)
    for r in range(N):
        k = np.zeros(C, int) if r == e[0] else rng.permutation(C) % 3
        a = x[r][:, :8, :3].copy()
        a[:, :, 2] = 0
        x[r][:, :8] = a[:, :, k]
        bm[r][:, :8] = bm[r][:, :8, :1].copy()
        bm[r][rng.permutation(8) < 3, :8] = 0
    x[e[1]] = 0
    u = d["u"].reshape(N, 8, 16, 128, 4)
    u[:, :, 8:, ::16] = 0
    for g in range(8):
        for h in range(8):
            if h != g: u[:, h, :, 16 * g] = 0
    w = np.array(f(rng, N, 128, 2048)).reshape(N, 8, 16, 4, 8, 16, 4)
    w[:, :, :, :, :, :8] = 0
    return {"x": x.reshape(N, 128, 4 * C), "bm": bm.reshape(N, 128, 4 * C), "u": u.reshape(N, 128, 512), "v": d["v"], **stored(anywhere(rng)), **weights(rng, w.reshape(N, 128, 2048))}
def setup_inputs_near(rng):
    d = numbers_of(rng)
    o = rng.permutation(N)
    x = d["x"].astype(np.float32).reshape(N, 8, 16, C, 4)
    bm = d["bm"].astype(np.float32).reshape(N, 8, 16, C, 4)
    u = d["u"].astype(np.float32).reshape(N, 128, 128, 4)
    u[:, :, ::16] = 0
    for z in (x, bm):
        z[:, :, 11:] = rng.integers(4, 8, (N, 8, 5, C, 4)) * rng.choice([-1.0, 1.0], (N, 8, 5, C, 4)) * 2.0 ** -20
        for i in (0, 8, 9, 10): z[:, :, i] = 0
    sg = signs(rng)
    for r in range(N):
        small = o[r] % 2 == 1
        e = 2.0 ** -30 if small else 2.0 ** -23
        k = 1.0 if o[r] % 4 == 0 else 2.0 ** -30
        s = np.arange(C) // 2 if o[r] // 2 % 2 == 0 else np.arange(C) % (C // 2) // 2
        digit = (s[:, None] >> np.arange(8)) & 1
        turn = rng.choice([-1.0, 1.0])
        for g in range(8):
            a = (digit - 1 if small and sg[r, g] < 0 else digit) * e * np.exp2(np.arange(8))
            x[r, g, 8] = a[:, :4]
            x[r, g, 9] = a[:, 4:]
            if not small: x[r, g, 0, :, 0] = sg[r, g]
            if g % 2:
                j = int(rng.integers(C // 4))
                x[r, g, 0, j, 0] = -2.0 ** 30
                x[r, g, 0, j + C // 2, 0] = -2.0 ** 30
            one = rng.choice([-1.0, 1.0])
            bm[r, g, 10, 0, 0] = one * (8 if small and g < 4 else 512) * e
            h = 16 * g
            u[r, h, h, 0] = k
            u[r, h + 8:h + 10, h] = k
            u[r, h + 10, h, 0] = one * (turn if g % 2 else -turn) * k
            if small and g < 2:
                bm[r, g, 10, 0, 1] = bm[r, g, 10, 0, 0]
                u[r, h + 10, h, 1] = -u[r, h + 10, h, 0]
                u[r, h + 10, h, 0] *= 1.125
    size = np.full(16, 32.0)
    size[[0, 8, 9, 10]] = 0
    return {"x": x.reshape(N, 128, 4 * C).astype(BF), "bm": bm.reshape(N, 128, 4 * C).astype(BF), "u": u.reshape(N, 128, 512).astype(BF), "v": d["v"], **stored(anywhere(rng)), **straight(rng, size)}
def setup_inputs_huge(rng):
    d = numbers_of(rng)
    o = rng.permutation(N)
    x = 2.0 ** 30 * (0.5 + 0.1 * rng.random((N, 128, C, 4)))
    c = np.stack([rng.permutation(C) % 2 * 2.0 - 1.0 for r in range(N)])
    c[o < N // 2] = 1
    x *= c[:, None, :, None]
    bm = 2.0 ** 27 * (0.5 + 0.5 * rng.random((N, 128, 4 * C))) * (o % 2 * 2.0 - 1.0)[:, None, None]
    u = d["u"].reshape(N, 128, 128, 4)
    a = 2.0 ** 30 * (1 - 0.25 * rng.random((N, 128, 8, 4))) * signs(rng)[:, None, :, None]
    u[:, :, ::16] = a.astype(np.float32).astype(BF)
    return {"x": x.astype(np.float32).reshape(N, 128, 4 * C).astype(BF), "bm": bm.astype(np.float32).astype(BF), "u": u.reshape(N, 128, 512), "v": d["v"], **stored(anywhere(rng)), **straight(rng, np.full(16, 4.0))}
def setup_inputs_coords(rng):
    a = anywhere(rng)
    i = np.arange(C)
    for r in range(N):
        g = rng.permutation(8)
        a[r, g[0]] = int(rng.integers(C))
        a[r, g[1]] = rng.permutation(C) % 2 * (C - 1)
        a[r, g[2]] = i
        a[r, g[3]] = C - 1 - i
        a[r, g[4]] = i % 2
    return {**numbers_of(rng), **stored(a), **weights(rng, f(rng, N, 128, 2048))}
def setup_inputs_spread(rng):
    d = setup_inputs(rng)
    d["x"] = big(wide(rng, N, 128, 4 * C, cols=6))
    d["bm"] = big(wide(rng, N, 128, 4 * C, cols=6))
    return d
def check_inputs(d):
    b = []
    for k in ("x", "bm", "u", "v"):
        a = np.abs(d[k].astype(np.float32))
        if not (np.isfinite(a).all() and ((a == 0) | (a >= 2.0 ** -30) & (a <= 2.0 ** 30)).all()): b.append("a value of " + k)
    for k in ("co", "cn"):
        if ((d[k] < 0) | (d[k] >= C)).any(): b.append("an entry of " + k)
    for r in range(N):
        e = np.concatenate([gentries(d["co"][(r + s) % N])[:, :T] for s in STEP], axis=1)
        if (gentries(d["cn"][r]) != e).any(): b.append("cn isn't what co of other ranks says")
    if (d["wc"] % 128 == 127).any(): b.append("a code of wc that is no number")
    for p in d["ws"]:
        s = mx_ref.live(p)
        if ((s < 1) | (s > 157)).any(): b.append("a scale of ws")
    return b
def reference(x, bm, u, v, co, cn, wc, ws):
    qu = [mx_ref.quantize(u[r]) for r in range(N)]
    lay = [pk(wc[r], ws[r]) for r in range(N)]
    now, beam = [x[r] for r in range(N)], [bm[r] for r in range(N)]
    half = C // 2
    ol = np.zeros((N, 8, 2 * R), np.float32)
    for t in range(R):
        left, sent = [], []
        for r in range(N):
            p = mx_ref.matmul(qu[r], mx_ref.quantize(now[r]))[::16] + np.float32(0.0)
            s = mx_ref.matmul(qu[r], mx_ref.quantize(np.ascontiguousarray(beam[r][:, :16])))[::16, 0]
            k = np.argmax(p.reshape(8, 2, half), axis=2) + np.array([0, half])
            best = np.take_along_axis(p, k, axis=1)
            h = np.where(best[:, 1] > best[:, 0], k[:, 1], k[:, 0])
            c = np.repeat(np.where(s > 0, np.float32(0.5), np.float32(-0.5)), 16)[:, None]
            own = gentries(co[r])
            far = gentries(cn[r])[:, T * t:T * t + T]
            e = np.abs(own - np.repeat(np.take_along_axis(own, k, axis=1), half, axis=1))
            left.append(now[r].astype(np.float32) - c * gcols(beam[r], e).astype(np.float32))
            e = np.abs(far - np.take_along_axis(own, h[:, None], axis=1))
            sent.append(mx_ref.quantize((c * gcols(beam[r], e).astype(np.float32)).astype(BF)))
            ol[r, :, 2 * t:2 * t + 2] = k
        for r in range(N):
            left[r][:, :4 * T] = left[r][:, :4 * T] - decode(sent[(r - STEP[t]) % N])
            now[r] = left[r].astype(BF)
            if t < R - 1:
                q = mx_ref.quantize(now[r])
                beam[r] = tile([mx_ref.matmul(pick(lay[r], np.arange(128 * b, 128 * b + 128)), q) * np.float32(0.015625) + beam[r][:, b::4].astype(np.float32) * np.float32(0.5) for b in range(4)])
    y = np.zeros((N, 128, C), np.float32)
    oc, osc = np.zeros((N, 128, 4 * C), np.uint8), np.zeros((N, 16, C), np.uint8)
    for r in range(N):
        q = mx_ref.quantize(now[r])
        y[r] = mx_ref.matmul(mx_ref.quantize(v[r]), q)
        oc[r], osc[r] = emit(q)
    return {"y": y, "ol": ol, "oc": oc, "osc": osc}

from concourse.mybir import dt, AluOpType, ActivationFunctionType

A, F = AluOpType, ActivationFunctionType
C, H, R = 384, 192, 3
STEP = [1, 2, 4]


def _scratch():
    s = {}

    def bf(n, w): s[n] = ("sbuf", [128, w], "bfloat16")
    def f32(n, w): s[n] = ("sbuf", [128, w], "float32")
    def i32(n, w): s[n] = ("sbuf", [128, w], "int32")
    def u16(n, w): s[n] = ("sbuf", [128, w], "uint16")

    def mx(n, w):
        s[n + "c"] = ("sbuf", [128, w], "float8_e4m3fn_x4")
        s[n + "s"] = ("sbuf", [128, w], "uint8")
    bf("ut", 512), bf("vt", 512), bf("bmt", 4 * C), bf("ones", 528), bf("diag", 528)
    for t in range(R + 1):
        bf("x%d" % t, 4 * C), mx("qx%d" % t, C)
    for t in range(R):
        bf("wn%d" % t, 4 * C), f32("e%d" % t, 4 * H), bf("tl%d" % t, 4 * H), mx("qt%d" % t, H), mx("ld%d" % t, H), mx("qb%d" % t, 128)
        f32("m%d" % t, C), bf("jk%d" % t, C), f32("na%d" % t, 48), f32("la%d" % t, 36), u16("lo%d" % t, 48), u16("ok%d" % t, 8)
        f32("sm%d" % t, 16), f32("cc%d" % t, 4)
    for t in (1, 2):
        bf("bp%d" % t, 4 * C), bf("bs%d" % t, 512), bf("hc%d" % t, 16)
    bf("h0", 4 * C), bf("h1", 4 * C), u16("lb", 64)
    mx("qu", 128), mx("qr", 128), mx("qv", 128), mx("qe", 512), mx("lay", 512)
    i32("cow", 24), i32("cnw", 36), f32("cof", 24), f32("cnf", 36), f32("rep", 768), f32("rept", 768), f32("nat", C)
    i32("ic", 24), i32("ip", 24), i32("im", 24), i32("isum", 24), u16("offn", 24), i32("iu", 8), u16("offu", 8), i32("ir", 48), u16("offr", 48)
    f32("low", H), f32("ko", 8), f32("kr", 4), f32("yb", C)
    for k in range(8):
        s["ps%d" % k] = ("psum", [128, 512], "float32")
    return s


SCRATCH = _scratch()
SEMAPHORES = ["sT", "sV", "sS", "sG", "dU", "dX0", "dX1", "dB0", "dB1", "dC", "dN", "dW", "dV", "dY", "snt"] + ["arr%d" % t for t in range(R)]


def rank_program(g, core, T, topo):
    rank = T.rank_of(core)
    if rank is None:
        return
    eng = {"T": g.tensor, "V": g.vector, "S": g.scalar, "G": g, "Y": g.sync}
    total = {}
    waited = {}
    clock = {q: {} for q in eng}
    writer, readers = {}, {}
    order = [0]

    def need(q, d):
        sem, val = d["sem"], (total[d["sem"]] if d["dma"] else d["val"])
        if clock[q].get(sem, 0) >= val:
            return
        eng[q].wait_ge(T.sem[sem], val)
        waited[sem] = max(waited.get(sem, 0), val)
        clock[q][sem] = val
        for k, v in d["snap"].items():
            clock[q][k] = max(clock[q].get(k, 0), v)

    def op(q, fn, rd=(), wr=(), sem=None, inc=None):
        dma = sem is not None
        deps = {}
        for k in rd:
            for d in writer.get(k, []):
                deps[d["n"]] = d
            if k.startswith("ps"):
                for d in readers.get(k, []):
                    if d["q"] != q: deps[d["n"]] = d
        for k in wr:
            if not readers.get(k):
                for d in writer.get(k, []):
                    if not (dma and d["sem"] == sem): deps[d["n"]] = d
            for d in readers.get(k, []):
                if d["q"] != q or d["dma"]: deps[d["n"]] = d
        for n in sorted(deps, reverse=True):
            need(q, deps[n])
        ins = fn()
        s = sem if dma else "s" + q
        step = (inc or 16) if dma else 1
        if inc is None:
            ins.then_inc(T.sem[s], step)
        total[s] = total.get(s, 0) + step
        order[0] += 1
        me = {"n": order[0], "q": q, "sem": s, "val": total[s], "dma": dma, "snap": dict(clock[q])}
        for k in rd:
            readers.setdefault(k, []).append(me)
        for k in wr:
            writer[k] = [d for d in writer.get(k, []) if dma and d["sem"] == s] + [me]
            readers[k] = []

    V, S, PE = g.vector, g.scalar, g.tensor
    part = {"l": (0, H), "u": (H, C)}

    def codes(n, a, b): return T[n + "c"][:, a:b]
    def plane(n, a, b): return T[n + "s"][:, a:b]

    def quant(n, a, b, tile, keys, wkey):
        op("V", lambda: V.quantize_mx(codes(n, a, b), plane(n, a, b), tile), keys, [wkey])

    def mm(bank, st, sa, mv, a, b, rd):
        k = "ps%d" % bank
        op("T", lambda: PE.matmul_mx(T[k][:, 0:b - a], codes(st, sa, sa + 128), plane(st, sa, sa + 128), codes(mv, a, b), plane(mv, a, b), True, True), rd, [k])

    def load(q, out, in_, key, sem): op(q, lambda: eng[q].dma_start(out, in_), [], [key], sem)

    QR = ["qrc", "qrs"]
    BM = ["bma", "bmb"]

    def qstate(t, h):
        a, b = part[h]
        quant("qx%d" % t, a, b, T["x%d" % t][:, 4 * a:4 * b], ["x%d%s" % (t, h)], "qx%d%s" % (t, h))

    def score(t, h, bank):
        a, b = part[h]
        mm(bank, "qr", 0, "qx%d" % t, a, b, QR + ["qx%d%s" % (t, h)])

    def scan(t, h, bank):
        a, b = part[h]
        op("V", lambda: V.tensor_tensor_scan(T["m%d" % t][:, a:b], T["ps%d" % bank][:, 0:H], T.low[:], -1.0e29, A.max, A.max), ["ps%d" % bank, "low"], ["m%d%s" % (t, h)])

    def count(t, h):
        a, b = part[h]
        m = T["m%d" % t]
        acc = T.ko[:, 2 * t:2 * t + 1] if h == "l" else T.kr[:, t:t + 1]
        op("S", lambda: S.activation(T["jk%d" % t][:, a:b], m[:, a:b], F.Sign, bias=m[:, b - 1:b], scale=-1.0, accum_out=acc), ["m%d%s" % (t, h)], ["k%d%s" % (t, h), "jk%d%s" % (t, h)])

    def look(t, i, col):
        op("S", lambda: S.activation(T["na%d" % t][:, 16 * i:16 * i + 16], T.nat[:, 0:C].indirect(T["ok%d" % t][:, col:col + 1]), F.Copy), ["nat", "ok%d%d" % (t, col)], ["na%d%d" % (t, i)])

    def dist(t, i, src, key):
        op("S", lambda: S.activation(T["la%d" % t][:, 12 * i:12 * i + 12], src, F.Abs, bias=T["na%d" % t][:, 16 * i:16 * i + 1], scale=1.0), [key, "na%d%d" % (t, i)], ["la%d%d" % (t, i)])

    def conv(t, i):
        op("V", lambda: V.tensor_copy(T["lo%d" % t][:, 16 * i:16 * i + 12], T["la%d" % t][:, 12 * i:12 * i + 12]), ["la%d%d" % (t, i)], ["lo%d%d" % (t, i)])

    def conv4(b):
        op("V", lambda: V.tensor_scalar(T.lb[:, 16 * b:16 * b + 12], T.la0[:, 0:12], 4.0, float(b), A.mult, A.add), ["la00"], ["lb%d" % b])

    def lst(t, i): return T["lo%d" % t][:, 16 * i:16 * i + 12]

    def facet1(t):
        op("V", lambda: V.tensor_scalar(T.ko[:, 2 * t + 1:2 * t + 2], T.kr[:, t:t + 1], float(H), None, A.add), ["k%du" % t], ["p%d" % t])
        op("V", lambda: V.tensor_scalar(T["ok%d" % t][:, 4:5], T.kr[:, t:t + 1], float(H), None, A.add), ["k%du" % t], ["ok%d4" % t])

    def list1(t):
        look(t, 2, 4)
        dist(t, 2, T.cof[:, 12:24], "cof")

    def select(t):
        m, s = T["m%d" % t], T["sm%d" % t]
        rd = ["m%du" % t, "m%dl" % t]
        op("V", lambda: V.tensor_scalar(s[:, 1:2], m[:, C - 1:C], m[:, H - 1:H], T.ko[:, 2 * t + 1:2 * t + 2], A.is_gt, A.mult), rd + ["p%d" % t], ["sm%db" % t])
        op("V", lambda: V.tensor_scalar(s[:, 0:1], m[:, C - 1:C], m[:, H - 1:H], None, A.is_le), rd, ["sm%da" % t])

    def choose(t):
        s = T["sm%d" % t]
        op("V", lambda: V.tensor_scalar(T["ok%d" % t][:, 0:1], T.ko[:, 2 * t:2 * t + 1], s[:, 0:1], s[:, 1:2], A.mult, A.add), ["k%dl" % t, "sm%da" % t, "sm%db" % t], ["ok%d0" % t])

    def off0(t):
        op("V", lambda: V.tensor_copy(T["ok%d" % t][:, 2:3], T.ko[:, 2 * t:2 * t + 1]), ["k%dl" % t], ["ok%d2" % t])

    def sign(t):
        cc = T["cc%d" % t]
        op("V", lambda: V.tensor_scalar(cc[:, 0:1], T.ps2[:, 0:1], 0.0, 0.5, A.is_gt, A.subtract), ["ps2"], ["c%d" % t])
        if t:
            op("V", lambda: V.tensor_scalar(cc[:, 1:2], cc[:, 0:1], 0.015625, None, A.mult), ["c%d" % t], ["ct%d" % t])

    def minus_sign(t):
        cc = T["cc%d" % t]
        op("V", lambda: V.tensor_scalar(cc[:, 2:3], cc[:, 0:1], -0.015625 if t else -1.0, None, A.mult), ["c%d" % t], ["cw%d" % t])

    def window(t, b, q):
        out, w = T["wn%d" % t][:, C * b:C * b + C], T["cc%d" % t][:, 2:3]
        src, keys = (T.bmt[:, b:4 * C:4], BM) if t == 0 else (T["bp%d" % t][:, C * b:C * b + C], ["bp%d%du" % (t, b), "bp%d%dl" % (t, b)])
        if q == "V":
            op("V", lambda: V.tensor_scalar(out, src, w, None, A.mult), keys + ["cw%d" % t], ["wn%d%d" % (t, b)])
        else:
            op("S", lambda: S.activation(out, src, F.Copy, scale=w), keys + ["cw%d" % t], ["wn%d%d" % (t, b)])

    def tail(t, b, q):
        out = T["tl%d" % t][:, b:4 * H:4]
        if t == 0:
            src, sc, keys = T.bmt[:, 0:4 * C].indirect(T.lb[:, 16 * b:16 * b + 12]), T.cc0[:, 0:1], BM + ["c0", "lb%d" % b]
        else:
            src, sc, keys = T["bp%d" % t][:, C * b:C * b + C].indirect(lst(t, 0)), T["cc%d" % t][:, 1:2], ["bp%d%du" % (t, b), "bp%d%dl" % (t, b), "ct%d" % t, "lo%d0" % t]
        if q == "V":
            op("V", lambda: V.tensor_scalar(out, src, sc, None, A.mult), keys, ["tl%d%d" % (t, b)])
        else:
            op("S", lambda: S.activation(out, src, F.Copy, scale=sc), keys, ["tl%d%d" % (t, b)])

    def send(t):
        dst = T.cores[(rank + STEP[t]) % len(T.cores)]
        rid, pid = topo.addr(dst)[0:2]
        mask, n = topo.mask(core, dst), len(topo.engines(core, dst))
        q, ld, arr = "qt%d" % t, "ld%d" % t, "arr%d" % t
        quant(q, 0, H, T["tl%d" % t][:], ["tl%d%d" % (t, b) for b in range(4)], q)
        for out, in_ in ((codes(ld, 0, H).bitcast(dt.uint8), codes(q, 0, H).bitcast(dt.uint8)), (plane(ld, 0, H), plane(q, 0, H))):
            op("G", lambda: g.remote_dma(out, in_, T.sem[arr], T.sem["snt"], pid, rid, mask), [q], [], "snt", n)
        src = T.cores[(rank - STEP[t]) % len(T.cores)]
        total[arr] = 2 * len(topo.engines(src, core))
        writer[ld] = [{"n": order[0], "q": "far", "sem": arr, "val": total[arr], "dma": True, "snap": {}}]

    def upper(t, b):
        op("V", lambda: V.tensor_tensor(T["x%d" % (t + 1)][:, 4 * H + b:4 * C:4], T["wn%d" % t][:, C * b:C * b + C].indirect(lst(t, 2)), T["x%d" % t][:, 4 * H + b:4 * C:4], A.add),
           ["wn%d%d" % (t, b), "lo%d2" % t, "x%du" % t], ["x%du%d" % (t + 1, b)])

    def lower(t, b):
        op("V", lambda: V.tensor_tensor(T["e%d" % t][:, H * b:H * b + H], T["wn%d" % t][:, C * b:C * b + C].indirect(lst(t, 1)), T["x%d" % t][:, b:4 * H:4], A.add),
           ["wn%d%d" % (t, b), "lo%d1" % t, "x%dl" % t], ["e%d%d" % (t, b)])

    def minus(t, b):
        op("V", lambda: V.tensor_tensor(T["x%d" % (t + 1)][:, b:4 * H:4], T["e%d" % t][:, H * b:H * b + H], T["ps%d" % b][:, 0:H], A.subtract),
           ["e%d%d" % (t, b), "ps%d" % b], ["x%dl%d" % (t + 1, b)])

    def join(k):
        writer[k] = [d for b in range(4) for d in writer["%s%d" % (k, b)]]

    def product(t, h, b):
        a, e = part[h]
        mm(4 + b, "lay", 128 * b, "qx%d" % t, a, e, ["lay", "qx%d%s" % (t, h)])

    def beam(t, h, b):
        a, e = part[h]
        op("V", lambda: V.tensor_tensor(T["bp%d" % t][:, C * b + a:C * b + e], T["ps%d" % (4 + b)][:, 0:H], T["h%d" % (t - 1)][:, C * b + a:C * b + e], A.add),
           ["ps%d" % (4 + b), "h%d%d" % (t - 1, b)], ["bp%d%d%s" % (t, b, h)])

    def column0(t, b):
        op("S", lambda: S.activation(T["bs%d" % t][:, b:b + 1], T["ps%d" % (4 + b)][:, 0:1], F.Identity, bias=T["hc%d" % t][:, b:b + 1], scale=0.015625),
           ["ps%d" % (4 + b), "hc%d" % t, "bz%d" % t], ["bs%d%d" % (t, b)])

    def half(t, b):
        src, keys, k = (T.bmt[:, b:4 * C:4], BM, 32.0) if t == 0 else (T.bp1[:, C * b:C * b + C], ["bp1%du" % b, "bp1%dl" % b], 0.5)
        op("S", lambda: S.activation(T["h%d" % t][:, C * b:C * b + C], src, F.Copy, scale=k), keys, ["h%d%d" % (t, b)])

    def halfcol(t):
        src, keys = (T.bmt[:, 0:4], ["bma"]) if t == 1 else (T.bs1[:, 0:4], ["bs1%d" % b for b in range(4)])
        op("S", lambda: S.activation(T["hc%d" % t][:, 0:4], src, F.Copy, scale=0.5), keys, ["hc%d" % t])

    def store(q, keys, out, in_): op(q, lambda: eng[q].dma_start(out, in_), keys, [], "dY")

    def emit(h):
        a, b = part[h]
        k = ["qx%d%s" % (R, h)]
        store("Y", k, T.oc[:, 4 * a:4 * b], codes("qx%d" % R, a, b).bitcast(dt.uint8))
        for i in range(4):
            store("S" if h == "l" else "Y", k, T.osc[4 * i:4 * i + 4, a:b], T["qx%ds" % R][32 * i:32 * i + 4, a:b])

    def result(h, bank):
        a, b = part[h]
        mm(bank, "qv", 0, "qx%d" % R, a, b, ["qv", "qx%d%s" % (R, h)])

    def yout(h, bank):
        a, b = part[h]
        op("V", lambda: V.tensor_copy(T.yb[:, a:b], T["ps%d" % bank][:, 0:H]), ["ps%d" % bank], ["yb" + h])
        store("Y", ["yb" + h], T.y[:, a:b], T.yb[:, a:b])

    load("S", T.cow[:], T.co[:, :], "cow", "dC")
    load("Y", T.ut[:], T.u[:, :], "ut", "dU")
    load("S", T.x0[:, 4 * H:], T.x[:, 4 * H:], "x0u", "dX1")
    load("Y", T.x0[:, 0:4 * H], T.x[:, 0:4 * H], "x0l", "dX0")
    load("S", T.cnw[:], T.cn[:, :], "cnw", "dN")
    load("Y", T.bmt[:, 0:512], T.bm[:, 0:512], "bma", "dB0")
    load("Y", T.bmt[:, 512:4 * C], T.bm[:, 512:4 * C], "bmb", "dB1")
    load("Y", codes("lay", 0, 512).bitcast(dt.uint8), T.wc[:, :], "lay", "dW")
    load("Y", plane("lay", 0, 512), T.ws[:, :], "lay", "dW")
    load("Y", T.vt[:], T.v[:, :], "vt", "dV")

    op("V", lambda: V.memset(T.ones[:], 1.0), [], ["ones"])
    op("G", lambda: g.iota(T.iu[:], [[16, 8]], 0, 0), [], ["iu"])
    op("G", lambda: g.iota(T.ir[:], [[1, 24], [0, 2]], 0, 0), [], ["ir"])
    op("G", lambda: g.affine_select(T.diag[:, 0:516], T.ones[:, 0:516], [[-1, 516]], A.is_equal, 0.0, 3, 4), ["ones"], ["diag"])
    op("G", lambda: g.iota(T.ic[:], [[32, 24]], 0, 0), [], ["ic"])
    op("G", lambda: g.iota(T.ip[:], [[0, 24]], 0, 1), [], ["ip"])
    op("V", lambda: V.memset(T.low[:], -1.0e29), [], ["low"])
    op("V", lambda: V.tensor_copy(T.offu[:], T.iu[:]), ["iu"], ["offu"])
    op("V", lambda: V.tensor_copy(T.offr[:], T.ir[:]), ["ir"], ["offr"])
    for t in (1, 2):
        op("V", lambda: V.memset(T["bs%d" % t][:], 0.0), [], ["bz%d" % t])
    for b in range(4):
        quant("qe", 128 * b, 128 * b + 128, T.diag[:, 3 - b:515 - b], ["diag"], "qe%d" % b)
    op("V", lambda: V.tensor_scalar(T.im[:], T.ip[:], 31, None, A.bitwise_and), ["ip"], ["im"])
    op("V", lambda: V.tensor_tensor(T.isum[:], T.im[:], T.ic[:], A.add), ["im", "ic"], ["isum"])
    op("V", lambda: V.tensor_copy(T.offn[:], T.isum[:]), ["isum"], ["offn"])

    op("V", lambda: V.tensor_copy(T.cof[:], T.cow[:]), ["cow"], ["cof"])
    quant("qu", 0, 128, T.ut[:], ["ut"], "qu")
    op("V", lambda: V.tensor_copy(codes("qr", 0, 128).bitcast(dt.uint32), codes("qu", 0, 128).bitcast(dt.uint32).indirect(T.offu[:, 0:8])), ["qu", "offu"], ["qrc"])
    op("S", lambda: S.activation(T.rep[:], T.cof[:, 0:24].indirect(T.offr[:, 0:48]), F.Copy), ["cof", "offr"], ["rep"])
    op("S", lambda: S.activation(plane("qr", 0, 128), plane("qu", 0, 128).indirect(T.offu[:, 0:8]), F.Copy), ["qu", "offu"], ["qrs"])

    qstate(0, "u")
    score(0, "u", 0)
    op("V", lambda: V.transpose(T.rept[:], T.rep[:]), ["rep"], ["rept"])
    qstate(0, "l")
    score(0, "l", 1)
    op("S", lambda: S.activation(T.nat[:], T.rept[:, 0:768].indirect(T.offn[:, 0:24]), F.Copy, scale=-1.0), ["rept", "offn"], ["nat"])
    scan(0, "u", 0)
    count(0, "u")
    scan(0, "l", 1)
    count(0, "l")
    op("V", lambda: V.tensor_copy(T.cnf[:], T.cnw[:]), ["cnw"], ["cnf"])
    facet1(0)
    select(0)
    choose(0)
    look(0, 0, 0)
    dist(0, 0, T.cnf[:, 0:12], "cnf")
    quant("qb0", 0, 128, T.bmt[:, 0:512], ["bma"], "qb0")
    mm(2, "qr", 0, "qb0", 0, 128, QR + ["qb0"])
    off0(0)
    for b in (0, 2, 1, 3):
        conv4(b)
    sign(0)
    tail(0, 0, "S")
    tail(0, 2, "V")
    tail(0, 1, "S")
    tail(0, 3, "V")
    list1(0)
    look(0, 1, 2)
    dist(0, 1, T.cof[:, 0:12], "cof")
    send(0)
    conv(0, 2)

    for t in range(R):
        n = t + 1
        minus_sign(t)
        window(t, 0, "V")
        window(t, 2, "S")
        window(t, 1, "V")
        window(t, 3, "S")
        if n < R:
            for b in range(4):
                half(t, b)
            halfcol(n)
        for b in range(4):
            upper(t, b)
        join("x%du" % n)
        qstate(n, "u")
        conv(t, 1)
        if n < R:
            score(n, "u", 0)
            for b in range(4):
                product(n, "u", b)
        else:
            quant("qv", 0, 128, T.vt[:], ["vt"], "qv")
            result("u", 4)
            emit("u")
        for b in range(4):
            lower(t, b)
        if n < R:
            scan(n, "u", 0)
            count(n, "u")
            for b in range(4):
                beam(n, "u", b)
            facet1(n)
            list1(n)
            conv(n, 2)
        else:
            yout("u", 4)
            store("Y", ["k%dl" % i for i in range(R)] + ["p%d" % i for i in range(R)], T.ol[:, :], T.ko[::16, 0:6])
        for b in range(4):
            mm(b, "qe", 128 * b, "ld%d" % t, 0, H, ["qe%d" % b, "ld%d" % t])
        for b in range(4):
            minus(t, b)
        join("x%dl" % n)
        qstate(n, "l")
        if n == R:
            result("l", 5)
            emit("l")
            yout("l", 5)
            break
        score(n, "l", 1)
        for b in range(4):
            product(n, "l", b)
        scan(n, "l", 1)
        count(n, "l")
        for b in range(4):
            column0(n, b)
        join("bs%d" % n)
        select(n)
        beam(n, "l", 0)
        choose(n)
        look(n, 0, 0)
        dist(n, 0, T.cnf[:, 12 * n:12 * n + 12], "cnf")
        quant("qb%d" % n, 0, 128, T["bs%d" % n][:], ["bs%d" % n], "qb%d" % n)
        mm(2, "qr", 0, "qb%d" % n, 0, 128, QR + ["qb%d" % n])
        beam(n, "l", 1)
        conv(n, 0)
        sign(n)
        beam(n, "l", 2)
        beam(n, "l", 3)
        tail(n, 0, "S")
        tail(n, 1, "S")
        tail(n, 2, "V")
        tail(n, 3, "V")
        send(n)
        off0(n)
        look(n, 1, 2)
        dist(n, 1, T.cof[:, 0:12], "cof")

    for s in sorted(total):
        if waited.get(s, 0) < total[s]:
            g.wait_ge(T.sem[s], total[s])
